import numpy as np, ml_dtypes
CORES = [32,33,40,41,48,49,56,57,64,65,72,73]
N = 12
ROWS, COLS = 3, 4
def setup_inputs(rng):
    return {"x": rng.standard_normal((N, 128, 256), dtype=np.float32).astype(ml_dtypes.bfloat16)}
def reference(x):
    g = x.astype(np.float64).reshape(ROWS, COLS, 128, 256)
    rs = g.sum(axis=1)
    cs = g.sum(axis=0)
    y1 = np.stack([rs[r // COLS] for r in range(N)]).astype(x.dtype)
    y2 = np.stack([cs[r % COLS] for r in range(N)]).astype(x.dtype)
    return {"y1": y1, "y2": y2}

from concourse.bass import DstId, RemoteDMATransfer

ADD = 1
ROW_HELPER = (2, 6)
COL_HELPER = (4, 5)
CUT = (0, 43, 86, 128)
WID = tuple(2 * (CUT[j + 1] - CUT[j]) for j in range(3))
ON_CHIP = 0xFFFF
OFF_CHIP = 0x00FF

SCRATCH = {
    "xr": ("dram", [2, 128, 128], "bfloat16"),
    "yr": ("dram", [2, 128, 128], "bfloat16"),
    "xc0": ("dram", [128, WID[0]], "bfloat16"),
    "xc1": ("dram", [128, WID[1]], "bfloat16"),
    "xc2": ("dram", [128, WID[2]], "bfloat16"),
    "yc0": ("dram", [128, WID[0]], "bfloat16"),
    "yc1": ("dram", [128, WID[1]], "bfloat16"),
    "yc2": ("dram", [128, WID[2]], "bfloat16"),
    "rin": ("dram", [2, 128, 128], "bfloat16"),
    "rpeer": ("dram", [128, 128], "bfloat16"),
    "cin0": ("dram", [3, 128, WID[0]], "bfloat16"),
    "cin1": ("dram", [3, 128, WID[1]], "bfloat16"),
    "cin2": ("dram", [3, 128, WID[2]], "bfloat16"),
}
SEMAPHORES = ["ldr", "ldc", "sent", "rin_in", "peer_in", "cin_in", "row_in", "col_in", "st"]


def rank_program(g, core, T, topo):
    chip, k = topo.chip(core), core % 8
    if chip < 4:
        return
    grow, parity = (chip - 4) // 2, chip & 1
    S = T.sem

    def dst(c):
        rid, pid, _se = topo.addr(c)
        return DstId(rid=rid, pnc=pid)

    def send(out_ap, in_ap, to, sem):
        m = topo.mask(core, to)
        rid, pid, _se = topo.addr(to)
        g.remote_dma(out_ap, in_ap, sem, S.sent, pid, rid, m)
        return 16 if m == ON_CHIP else 8

    if k in (0, 1):
        g.sync.dma_start(T.xr[:], T.x[:]).then_inc(S.ldr, 16)
        for j in range(3):
            q = g.scalar if j < 2 else g.sync
            q.dma_start(T["xc%d" % j][:], T.x[CUT[j]:CUT[j + 1], :]).then_inc(S.ldc, 16)
        sent = 0
        g.wait_ge(S.ldr, 16)
        for h in range(2):
            sent += send(T.rin[k], T.xr[h], chip * 8 + ROW_HELPER[h], S.rin_in)
        g.wait_ge(S.ldc, 48)
        for j in range(3):
            to = (4 + 2 * j + parity) * 8 + COL_HELPER[k]
            sent += send(T["cin%d" % j][grow], T["xc%d" % j][:], to, S.cin_in)
        g.scalar.wait_ge(S.col_in, 24)
        for j in range(3):
            g.scalar.dma_start(T.y2[CUT[j]:CUT[j + 1], :], T["yc%d" % j][:]).then_inc(S.st, 16)
        g.sync.wait_ge(S.row_in, 32)
        g.sync.dma_start(T.y1[:], T.yr[:]).then_inc(S.st, 16)
        g.wait_ge(S.sent, sent)
        g.wait_ge(S.st, 64)

    elif k in ROW_HELPER:
        h = ROW_HELPER.index(k)
        g.wait_ge(S.rin_in, 32)
        g.remote_dma_fused([RemoteDMATransfer(
            dst_ids=[dst((chip ^ 1) * 8 + k)], dma_engine_mask=OFF_CHIP, remote_sem=S.peer_in,
            srcs=[T.rin[0], T.rin[1]], dsts=[T.rpeer[:]], alu_op=ADD)], local_sem=S.sent)
        g.wait_ge(S.peer_in, 8)
        g.remote_dma_fused([RemoteDMATransfer(
            dst_ids=[dst(chip * 8), dst(chip * 8 + 1)], dma_engine_mask=ON_CHIP, remote_sem=S.row_in,
            srcs=[T.rin[0], T.rin[1], T.rpeer[:]], dsts=[T.yr[h], T.yr[h]], alu_op=ADD)], local_sem=S.sent)
        g.wait_ge(S.sent, 8 + 16)

    elif k in COL_HELPER:
        kk = COL_HELPER.index(k)
        cin, yc = T["cin%d" % grow], T["yc%d" % grow]
        g.wait_ge(S.cin_in, 16 + 8 + 8)
        ranks = [(4 + 2 * i + parity) * 8 + kk for i in range(3)]
        g.remote_dma_fused([RemoteDMATransfer(
            dst_ids=[dst(c) for c in ranks], dma_engine_mask=OFF_CHIP, remote_sem=S.col_in,
            srcs=[cin[0], cin[1], cin[2]], dsts=[yc[:] for _c in ranks], alu_op=ADD)], local_sem=S.sent)
        g.wait_ge(S.sent, 8)
